import numpy as np
import ml_dtypes


def mxq(x, axis, fmt="e4m3"):
    dtype, down = {"e4m3": (ml_dtypes.float8_e4m3fn, 7), "e5m2": (ml_dtypes.float8_e5m2, 14)}[fmt]
    v = np.moveaxis(np.asarray(x, np.float32).astype(ml_dtypes.bfloat16).astype(np.float64), axis, -1)
    blocks = v.reshape(v.shape[:-1] + (-1, 32))
    amax = np.abs(blocks).max(-1, keepdims=True)
    byte = np.maximum(np.where(amax > 0, np.frexp(amax)[1] - 1 + 127, 0) - down, 1)
    scale = np.exp2(byte - 127.0)
    codes = (blocks / scale).astype(np.float32).astype(dtype).astype(np.float64)
    return np.moveaxis((codes * scale).reshape(v.shape), -1, axis)


WIDE = False


def mx_kscale(k):
    if not WIDE:
        return np.ones(k)
    levels = np.array([10, -10, 5, -5, 0])
    if k % 512:
        return np.exp2(np.random.permutation(np.resize(levels, k // 32))).repeat(32)
    a = np.empty((k // 512, 16))
    for p in range(k // 512):
        a[p, :8] = np.random.permutation(np.resize(levels, 8))
        for g in range(8):
            far = levels[np.abs(levels - a[p, g]) >= 10]
            a[p, g + 8] = far[np.random.randint(len(far))]
    return np.exp2(a.ravel()).repeat(32)


BF16 = ml_dtypes.bfloat16


def bf(x):
    return np.asarray(x, np.float32).astype(BF16)


def f64(x):
    return np.asarray(x).astype(np.float64)


E2M1 = np.array([0.0, 0.5, 1.0, 1.5, 2.0, 3.0, 4.0, 6.0, -0.0, -0.5, -1.0, -1.5, -2.0, -3.0, -4.0, -6.0])


def pack_weight(w, fmt):
    k, n = w.shape
    w = f64(bf(w)).reshape(k // 32, 32, n)
    amax = np.abs(w).max(1)
    if fmt == "e4m3":
        byte = np.frexp(amax)[1] - 1 + 127 - 7
    else:
        mant, ex = np.frexp(amax / 6.0)
        byte = np.where(mant > 0.5, ex, ex - 1) + 127
    byte = np.clip(np.where(amax > 0, byte, 1), 1, 254)
    scaled = (w * np.exp2(127.0 - byte)[:, None, :]).reshape(k, n).astype(np.float32)
    by_word = np.ascontiguousarray(scaled.reshape(k // 512, 128, 4, n).transpose(0, 1, 3, 2))
    if fmt == "e4m3":
        words = by_word.astype(ml_dtypes.float8_e4m3fn).view(np.uint8)
    else:
        c = by_word.astype(ml_dtypes.float4_e2m1fn).view(np.uint8) & 0xF
        words = c[..., 0::2] | (c[..., 1::2] << 4)
    return np.ascontiguousarray(words), np.ascontiguousarray(byte.astype(np.uint8).reshape(k // 512, 16, n))


def unpack_weight(words, scales, fmt):
    g, p, n, _ = words.shape
    if fmt == "e4m3":
        vals = np.ascontiguousarray(words).view(ml_dtypes.float8_e4m3fn).astype(np.float64)
    else:
        nib = np.empty((g, p, n, 4), np.uint8)
        nib[..., 0::2] = words & 0xF
        nib[..., 1::2] = words >> 4
        vals = E2M1[nib]
    vals = vals * np.repeat(np.exp2(scales.astype(np.float64) - 127.0), 8, axis=1)[..., None]
    return vals.transpose(0, 1, 3, 2).reshape(g * 512, n)
def pack4(w):
    words, scales = pack_weight(w, "e2m1")
    return words.reshape(words.shape[0], 128, -1), scales


def unpack4(words, scales):
    return unpack_weight(words.reshape(words.shape[0], 128, -1, 2), scales, "e2m1")


M, N = 512, 1536
DAMP = 1.0 / 3.0


def setup_inputs():
    s = mx_kscale(N)
    raw = np.random.standard_normal((N, N))
    b = DAMP * (raw + raw.T) / np.sqrt(2 * N)
    a_words, a_scales = pack4(b / s[:, None] * s)
    return {"x": bf(np.random.standard_normal((M, N)) * s),
            "a_words": a_words,
            "a_scales": a_scales,
            "g": bf((1 + 0.1 * np.random.standard_normal(N)) / s)}


def reference(x, a_words, a_scales, g):
    x0, gain = f64(x), f64(g)
    a = unpack4(a_words, a_scales)
    x1 = x0 + (mxq(x0, 1, "e4m3") @ a)
    x2 = x1 + (mxq(x1, 1, "e4m3") @ a)
    move = (mxq(x2, 1, "e4m3") @ a) * gain
    y = x2 * gain + move
    return y, move

@@ -1,0 +1,293 @@
+from contextlib import ExitStack
+
+import concourse.mybir as mybir
+from concourse.masks import make_identity
+
+M, N = 512, 1536
+FLOPS = 3 * 2 * M * N * N
+
+F32 = mybir.dt.float32
+BF16 = mybir.dt.bfloat16
+I32 = mybir.dt.int32
+U32 = mybir.dt.uint32
+U8 = mybir.dt.uint8
+FP8X4 = mybir.dt.float8_e4m3fn_x4
+FP4X4 = mybir.dt.float4_e2m1fn_x4
+ADD = mybir.AluOpType.add
+MULT = mybir.AluOpType.mult
+
+P = 128
+W = 512
+G = N // W
+TILES = M // P
+
+ORDER = [(0, 1), (1, 1), (2, 1), (0, 2), (1, 2), (3, 1), (0, 3), (2, 2), (1, 3), (3, 2), (2, 3), (3, 3)]
+FORM = ["TTT","TTT","TTT","TTT"]
+
+
+def tile_shifted_power_steps_t2_kernel(tc, x, a_words, a_scales, g, out_0, out_1):
+    nc = tc.nc
+    with ExitStack() as ctx:
+        keep = ctx.enter_context(tc.tile_pool(name="keep", bufs=1))
+        work = ctx.enter_context(tc.tile_pool(name="work", bufs=1))
+        acc_pool = ctx.enter_context(tc.psum_pool(name="acc", bufs=6))
+        turn_pool = ctx.enter_context(tc.psum_pool(name="turn", bufs=2))
+        ctx.enter_context(tc.manual_schedule())
+
+        ident = keep.tile([P, P], F32, name="ident")
+        a_plane = keep.tile([P, G * N], U8, name="a_plane", align_bytes=64)
+        a_codes = [keep.tile([P, 2 * N], U8, name="a_codes%d" % k, align_bytes=64) for k in range(G)]
+        x_raw = [keep.tile([P, N], BF16, name="x_raw%d" % i) for i in range(TILES)]
+        g_nat = keep.tile([P, N], BF16, name="g_nat")
+        g_sorted = {}
+        warm = keep.tile([P, 8], F32, name="warm")
+        warm2 = keep.tile([P, 8], F32, name="warm2")
+
+        nc.gpsimd.memset(warm[:], 0.0)
+        make_identity(nc, ident[:])
+        nc.scalar.copy(out=warm2[:], in_=warm[:])
+        nc.vector.memset(a_plane[:].bitcast(I32), 0)
+
+        def load_x(i):
+            nc.sync.dma_start(out=x_raw[i][:], in_=x[i * P : (i + 1) * P, :])
+
+        def load_a(k):
+            nc.sync.dma_start(out=a_codes[k][:].bitcast(I32), in_=a_words[k].bitcast(I32))
+
+        load_x(0)
+        scale_rows = a_scales.bitcast(I32).rearrange("k (q r) n -> r q k n", r=4)
+        for r in range(4):
+            nc.sync.dma_start(
+                out=a_plane[r:P:32, :].bitcast(I32).rearrange("q (k n) -> q k n", k=G), in_=scale_rows[r]
+            )
+        load_a(0)
+        load_x(1)
+        load_a(1)
+        load_a(2)
+        load_x(2)
+        load_x(3)
+        nc.sync.dma_start(out=g_nat[:], in_=g.partition_broadcast(P))
+
+        def sort_words(dst, src):
+            nc.vector.tensor_copy(
+                out=dst.bitcast(F32).rearrange("t (u p) -> t u p", u=2),
+                in_=src.bitcast(F32).rearrange("t (p u) -> t u p", u=2),
+            )
+
+        rounded = {}
+        resid = {}
+        turned = {}
+        grouped = {}
+        codes = {}
+        scales = {}
+        acc = {}
+        x2g = {}
+        move = {}
+
+        def sort_x(i):
+            for c in range(G):
+                t = work.tile([P, W], BF16, name="x_sorted", bufs=TILES * G)
+                sort_words(t[:], x_raw[i][:, c * W : (c + 1) * W])
+                rounded[(i, 1, c)] = t
+                resid[(i, 1, c)] = t
+
+        def transposes(n):
+            i, s = ORDER[n]
+            banks = [turn_pool.tile([P, 4, P], F32, name="turn") for h in range(2)]
+            turned[n] = banks
+            for k in range(G):
+                words = rounded[(i, s, k)][:].bitcast(F32)
+                for u in range(2):
+                    nc.tensor.transpose(banks[k // 2][:, 2 * (k % 2) + u, :], words[:, u * P : (u + 1) * P], ident[:])
+
+        def copy_out(n, h):
+            groups = 2 - h
+            t = work.tile([P, groups * W], BF16, name="grouped%d" % h, bufs=2, align_bytes=64)
+            grouped[(n, h)] = t
+            nc.scalar.copy(
+                out=t[:].bitcast(F32).rearrange("p (k r u) -> p k r u", k=groups, u=2),
+                in_=turned[n][h][:, 0 : 2 * groups, :].rearrange("p (k u) r -> p k r u", u=2),
+            )
+
+        def quantize(n, h):
+            groups = 2 - h
+            cd = work.tile([P, groups * P], U32, name="codes%d" % h, bufs=3, align_bytes=64)
+            sc = work.tile([P, groups * P], U8, name="scales%d" % h, bufs=3, align_bytes=64)
+            nc.vector.quantize_mx(out=cd[:].bitcast(FP8X4), scales=sc[:], in_=grouped[(n, h)][:])
+            for j in range(groups):
+                codes[(n, 2 * h + j)] = cd[:, j * P : (j + 1) * P]
+                scales[(n, 2 * h + j)] = sc[:, j * P : (j + 1) * P]
+
+        def mx_pass(n, c, k):
+            if k == 0:
+                acc[(n, c)] = acc_pool.tile([P, W], F32, name="acc")
+            nc.tensor.matmul_mx(
+                out=acc[(n, c)][:],
+                lhsT=codes[(n, k)].bitcast(FP8X4),
+                lhsT_scale=scales[(n, k)],
+                rhs=a_codes[k][:, 2 * W * c : 2 * W * (c + 1)].bitcast(FP4X4),
+                rhs_scale=a_plane[:, k * N + c * W : k * N + (c + 1) * W],
+                start=(k == 0),
+                stop=(k == G - 1),
+            )
+
+        def mm(n, c):
+            for k in range(G):
+                mx_pass(n, c, k)
+
+        def evac(n, c):
+            i, s = ORDER[n]
+            if s < 3:
+                t = work.tile([P, W], F32, name="iterate", bufs=15)
+                nc.vector.tensor_tensor(
+                    out=t[:].rearrange("t (u p e) -> t u p e", u=2, e=2),
+                    in0=acc[(n, c)][:].rearrange("t (p u e) -> t u p e", u=2, e=2),
+                    in1=resid[(i, s, c)][:].rearrange("t (u p e) -> t u p e", u=2, e=2),
+                    op=ADD,
+                )
+                resid[(i, s + 1, c)] = t
+            else:
+                t = work.tile([P, W], F32, name="move", bufs=6)
+                nc.vector.tensor_tensor(out=t[:], in0=acc[(n, c)][:], in1=g_nat[:, c * W : (c + 1) * W], op=MULT)
+                move[(i, c)] = t
+                nc.sync.dma_start(out=out_1[i * P : (i + 1) * P, c * W : (c + 1) * W], in_=t[:])
+
+        def round_bf16(n, c):
+            i, s = ORDER[n]
+            if s < 3:
+                t = work.tile([P, W], BF16, name="rounded", bufs=9)
+                nc.scalar.copy(out=t[:], in_=resid[(i, s + 1, c)][:])
+                rounded[(i, s + 1, c)] = t
+
+        ys = {}
+        x3s = {}
+
+        def store_y(n, c):
+            i, s = ORDER[n]
+            if s == 3:
+                nc.sync.dma_start(out=out_0[i * P : (i + 1) * P, c * W : (c + 1) * W], in_=ys[(i, c)][:])
+
+        def feed(n, c):
+            i, s = ORDER[n]
+            f = FORM[i][c]
+            cols = slice(c * W, (c + 1) * W)
+            if s == 3 and f in "TU":
+                y = work.tile([P, W], F32, name="y", bufs=6)
+                ys[(i, c)] = y
+                t = work.tile([P, W], F32, name="x3", bufs=6)
+                nc.vector.tensor_tensor(
+                    out=t[:].rearrange("t (p u e) -> t p u e", u=2, e=2),
+                    in0=acc[(n, c)][:].rearrange("t (p u e) -> t p u e", u=2, e=2),
+                    in1=resid[(i, 3, c)][:].rearrange("t (u p e) -> t p u e", u=2, e=2),
+                    op=ADD,
+                )
+                x3s[(i, c)] = t
+                if f == "T":
+                    nc.gpsimd.tensor_tensor(out=y[:], in0=t[:], in1=g_nat[:, cols], op=MULT)
+
+        def scale_x2(n, c):
+            i, s = ORDER[n]
+            f = FORM[i][c]
+            if s == 2 and f == "G":
+                t = work.tile([P, W], F32, name="x2g", bufs=6)
+                nc.gpsimd.tensor_tensor(out=t[:], in0=resid[(i, 3, c)][:], in1=g_sorted[c][:], op=MULT)
+                x2g[(i, c)] = t[:].rearrange("t (u p e) -> t p u e", u=2, e=2)
+            if s == 2 and f == "V":
+                t = work.tile([P, W], F32, name="x2g", bufs=6)
+                nc.vector.tensor_tensor(out=t[:], in0=resid[(i, 3, c)][:], in1=g_sorted[c][:], op=MULT)
+                x2g[(i, c)] = t[:].rearrange("t (u p e) -> t p u e", u=2, e=2)
+
+        def sum_y(n, c):
+            i, s = ORDER[n]
+            f = FORM[i][c]
+            if s == 3 and f == "U":
+                nc.vector.tensor_tensor(out=ys[(i, c)][:], in0=x3s[(i, c)][:], in1=g_nat[:, c * W : (c + 1) * W], op=MULT)
+            if s == 3 and f in "GV":
+                y = work.tile([P, W], F32, name="y", bufs=6)
+                ys[(i, c)] = y
+                nc.vector.tensor_tensor(
+                    out=y[:].rearrange("t (p u e) -> t p u e", u=2, e=2),
+                    in0=x2g[(i, c)],
+                    in1=move[(i, c)][:].rearrange("t (p u e) -> t p u e", u=2, e=2),
+                    op=ADD,
+                )
+
+        slots = len(ORDER)
+        sort_x(0)
+        transposes(0)
+        copy_out(0, 0)
+        copy_out(0, 1)
+        quantize(0, 0)
+        quantize(0, 1)
+        sort_x(1)
+        for c in range(G):
+            mx_pass(0, c, 0)
+        transposes(1)
+        copy_out(1, 0)
+        copy_out(1, 1)
+        for c in range(G):
+            for k in range(1, G):
+                mx_pass(0, c, k)
+        quantize(1, 0)
+        quantize(1, 1)
+        sort_x(2)
+        evac(0, 0)
+        round_bf16(0, 0)
+        evac(0, 1)
+        for n in range(1, slots):
+            more = n + 1 < slots
+            late = more and ORDER[n + 1][0] == ORDER[n - 1][0]
+            prev_late = n >= 2 and ORDER[n][0] == ORDER[n - 2][0]
+            if more and not late:
+                transposes(n + 1)
+                copy_out(n + 1, 0)
+                copy_out(n + 1, 1)
+            evac(n - 1, 2)
+            round_bf16(n - 1, 1)
+            round_bf16(n - 1, 2)
+            sum_y(n - 1, 1)
+            if FORM[ORDER[n - 1][0]][1] != "T":
+                store_y(n - 1, 1)
+            mm(n, 0)
+            if more and not late:
+                quantize(n + 1, 0)
+                quantize(n + 1, 1)
+            for c in range(G):
+                scale_x2(n - 1, c)
+            feed(n - 1, 2)
+            sum_y(n - 1, 2)
+            store_y(n - 1, 2)
+            if n == 1:
+                sort_x(3)
+            feed(n, 0)
+            evac(n, 0)
+            if FORM[ORDER[n][0]][0] == "T":
+                store_y(n, 0)
+            round_bf16(n, 0)
+            mm(n, 1)
+            if late:
+                transposes(n + 1)
+                copy_out(n + 1, 0)
+                copy_out(n + 1, 1)
+                evac(n, 1)
+                mm(n, 2)
+                quantize(n + 1, 0)
+                quantize(n + 1, 1)
+                feed(n, 1)
+            else:
+                feed(n, 1)
+                evac(n, 1)
+                mm(n, 2)
+            if FORM[ORDER[n][0]][1] == "T":
+                store_y(n, 1)
+            sum_y(n, 0)
+            if FORM[ORDER[n][0]][0] != "T":
+                store_y(n, 0)
+        n = slots
+        feed(n - 1, 2)
+        evac(n - 1, 2)
+        sum_y(n - 1, 1)
+        if FORM[ORDER[n - 1][0]][1] != "T":
+            store_y(n - 1, 1)
+        sum_y(n - 1, 2)
+        store_y(n - 1, 2)

@@ -22,7 +22,6 @@ G = N // W
 TILES = M // P
 
 ORDER = [(0, 1), (1, 1), (2, 1), (0, 2), (1, 2), (3, 1), (0, 3), (2, 2), (1, 3), (3, 2), (2, 3), (3, 3)]
-FORM = ["TTT","TTT","TTT","TTT"]
 
 
 def tile_shifted_power_steps_t2_kernel(tc, x, a_words, a_scales, g, out_0, out_1):
@@ -35,18 +34,20 @@ def tile_shifted_power_steps_t2_kernel(tc, x, a_words, a_scales, g, out_0, out_1
         ctx.enter_context(tc.manual_schedule())
 
         ident = keep.tile([P, P], F32, name="ident")
-        a_plane = keep.tile([P, G * N], U8, name="a_plane", align_bytes=64)
+        a_plane0 = keep.tile([P, N], U8, name="a_plane0", align_bytes=64)
+        a_plane12 = keep.tile([P, 2 * N], U8, name="a_plane12", align_bytes=64)
+        a_plane = [a_plane0[:], a_plane12[:, 0:N], a_plane12[:, N : 2 * N]]
         a_codes = [keep.tile([P, 2 * N], U8, name="a_codes%d" % k, align_bytes=64) for k in range(G)]
         x_raw = [keep.tile([P, N], BF16, name="x_raw%d" % i) for i in range(TILES)]
         g_nat = keep.tile([P, N], BF16, name="g_nat")
-        g_sorted = {}
         warm = keep.tile([P, 8], F32, name="warm")
         warm2 = keep.tile([P, 8], F32, name="warm2")
 
         nc.gpsimd.memset(warm[:], 0.0)
         make_identity(nc, ident[:])
         nc.scalar.copy(out=warm2[:], in_=warm[:])
-        nc.vector.memset(a_plane[:].bitcast(I32), 0)
+        nc.vector.memset(a_plane0[:].bitcast(I32), 0)
+        nc.vector.memset(a_plane12[:].bitcast(I32), 0)
 
         def load_x(i):
             nc.sync.dma_start(out=x_raw[i][:], in_=x[i * P : (i + 1) * P, :])
@@ -57,11 +58,13 @@ def tile_shifted_power_steps_t2_kernel(tc, x, a_words, a_scales, g, out_0, out_1
         load_x(0)
         scale_rows = a_scales.bitcast(I32).rearrange("k (q r) n -> r q k n", r=4)
         for r in range(4):
-            nc.sync.dma_start(
-                out=a_plane[r:P:32, :].bitcast(I32).rearrange("q (k n) -> q k n", k=G), in_=scale_rows[r]
-            )
+            nc.sync.dma_start(out=a_plane0[r:P:32, :].bitcast(I32), in_=scale_rows[r][:, 0, :])
         load_a(0)
         load_x(1)
+        for r in range(4):
+            nc.sync.dma_start(
+                out=a_plane12[r:P:32, :].bitcast(I32).rearrange("q (k n) -> q k n", k=2), in_=scale_rows[r][:, 1:G, :]
+            )
         load_a(1)
         load_a(2)
         load_x(2)
@@ -81,8 +84,8 @@ def tile_shifted_power_steps_t2_kernel(tc, x, a_words, a_scales, g, out_0, out_1
         codes = {}
         scales = {}
         acc = {}
-        x2g = {}
-        move = {}
+        x3 = {}
+        y = {}
 
         def sort_x(i):
             for c in range(G):
@@ -98,10 +101,10 @@ def tile_shifted_power_steps_t2_kernel(tc, x, a_words, a_scales, g, out_0, out_1
             for k in range(G):
                 words = rounded[(i, s, k)][:].bitcast(F32)
                 for u in range(2):
-                    nc.tensor.transpose(banks[k // 2][:, 2 * (k % 2) + u, :], words[:, u * P : (u + 1) * P], ident[:])
+                    nc.tensor.transpose(banks[min(k, 1)][:, 2 * (k // 2) + u, :], words[:, u * P : (u + 1) * P], ident[:])
 
         def copy_out(n, h):
-            groups = 2 - h
+            groups = 1 + h
             t = work.tile([P, groups * W], BF16, name="grouped%d" % h, bufs=2, align_bytes=64)
             grouped[(n, h)] = t
             nc.scalar.copy(
@@ -110,13 +113,13 @@ def tile_shifted_power_steps_t2_kernel(tc, x, a_words, a_scales, g, out_0, out_1
             )
 
         def quantize(n, h):
-            groups = 2 - h
+            groups = 1 + h
             cd = work.tile([P, groups * P], U32, name="codes%d" % h, bufs=3, align_bytes=64)
             sc = work.tile([P, groups * P], U8, name="scales%d" % h, bufs=3, align_bytes=64)
             nc.vector.quantize_mx(out=cd[:].bitcast(FP8X4), scales=sc[:], in_=grouped[(n, h)][:])
             for j in range(groups):
-                codes[(n, 2 * h + j)] = cd[:, j * P : (j + 1) * P]
-                scales[(n, 2 * h + j)] = sc[:, j * P : (j + 1) * P]
+                codes[(n, h + j)] = cd[:, j * P : (j + 1) * P]
+                scales[(n, h + j)] = sc[:, j * P : (j + 1) * P]
 
         def mx_pass(n, c, k):
             if k == 0:
@@ -126,7 +129,7 @@ def tile_shifted_power_steps_t2_kernel(tc, x, a_words, a_scales, g, out_0, out_1
                 lhsT=codes[(n, k)].bitcast(FP8X4),
                 lhsT_scale=scales[(n, k)],
                 rhs=a_codes[k][:, 2 * W * c : 2 * W * (c + 1)].bitcast(FP4X4),
-                rhs_scale=a_plane[:, k * N + c * W : k * N + (c + 1) * W],
+                rhs_scale=a_plane[k][:, c * W : (c + 1) * W],
                 start=(k == 0),
                 stop=(k == G - 1),
             )
@@ -149,7 +152,6 @@ def tile_shifted_power_steps_t2_kernel(tc, x, a_words, a_scales, g, out_0, out_1
             else:
                 t = work.tile([P, W], F32, name="move", bufs=6)
                 nc.vector.tensor_tensor(out=t[:], in0=acc[(n, c)][:], in1=g_nat[:, c * W : (c + 1) * W], op=MULT)
-                move[(i, c)] = t
                 nc.sync.dma_start(out=out_1[i * P : (i + 1) * P, c * W : (c + 1) * W], in_=t[:])
 
         def round_bf16(n, c):
@@ -159,21 +161,9 @@ def tile_shifted_power_steps_t2_kernel(tc, x, a_words, a_scales, g, out_0, out_1
                 nc.scalar.copy(out=t[:], in_=resid[(i, s + 1, c)][:])
                 rounded[(i, s + 1, c)] = t
 
-        ys = {}
-        x3s = {}
-
-        def store_y(n, c):
+        def add_x3(n, c):
             i, s = ORDER[n]
             if s == 3:
-                nc.sync.dma_start(out=out_0[i * P : (i + 1) * P, c * W : (c + 1) * W], in_=ys[(i, c)][:])
-
-        def feed(n, c):
-            i, s = ORDER[n]
-            f = FORM[i][c]
-            cols = slice(c * W, (c + 1) * W)
-            if s == 3 and f in "TU":
-                y = work.tile([P, W], F32, name="y", bufs=6)
-                ys[(i, c)] = y
                 t = work.tile([P, W], F32, name="x3", bufs=6)
                 nc.vector.tensor_tensor(
                     out=t[:].rearrange("t (p u e) -> t p u e", u=2, e=2),
@@ -181,36 +171,18 @@ def tile_shifted_power_steps_t2_kernel(tc, x, a_words, a_scales, g, out_0, out_1
                     in1=resid[(i, 3, c)][:].rearrange("t (u p e) -> t p u e", u=2, e=2),
                     op=ADD,
                 )
-                x3s[(i, c)] = t
-                if f == "T":
-                    nc.gpsimd.tensor_tensor(out=y[:], in0=t[:], in1=g_nat[:, cols], op=MULT)
+                x3[(n, c)] = t
 
-        def scale_x2(n, c):
-            i, s = ORDER[n]
-            f = FORM[i][c]
-            if s == 2 and f == "G":
-                t = work.tile([P, W], F32, name="x2g", bufs=6)
-                nc.gpsimd.tensor_tensor(out=t[:], in0=resid[(i, 3, c)][:], in1=g_sorted[c][:], op=MULT)
-                x2g[(i, c)] = t[:].rearrange("t (u p e) -> t p u e", u=2, e=2)
-            if s == 2 and f == "V":
-                t = work.tile([P, W], F32, name="x2g", bufs=6)
-                nc.vector.tensor_tensor(out=t[:], in0=resid[(i, 3, c)][:], in1=g_sorted[c][:], op=MULT)
-                x2g[(i, c)] = t[:].rearrange("t (u p e) -> t p u e", u=2, e=2)
+        def scale_y(engine, n, c):
+            if ORDER[n][1] == 3:
+                t = work.tile([P, W], F32, name="y", bufs=6)
+                engine.tensor_tensor(out=t[:], in0=x3[(n, c)][:], in1=g_nat[:, c * W : (c + 1) * W], op=MULT)
+                y[(n, c)] = t
 
-        def sum_y(n, c):
+        def store_y(n, c):
             i, s = ORDER[n]
-            f = FORM[i][c]
-            if s == 3 and f == "U":
-                nc.vector.tensor_tensor(out=ys[(i, c)][:], in0=x3s[(i, c)][:], in1=g_nat[:, c * W : (c + 1) * W], op=MULT)
-            if s == 3 and f in "GV":
-                y = work.tile([P, W], F32, name="y", bufs=6)
-                ys[(i, c)] = y
-                nc.vector.tensor_tensor(
-                    out=y[:].rearrange("t (p u e) -> t p u e", u=2, e=2),
-                    in0=x2g[(i, c)],
-                    in1=move[(i, c)][:].rearrange("t (p u e) -> t p u e", u=2, e=2),
-                    op=ADD,
-                )
+            if s == 3:
+                nc.sync.dma_start(out=out_0[i * P : (i + 1) * P, c * W : (c + 1) * W], in_=y[(n, c)][:])
 
         slots = len(ORDER)
         sort_x(0)
@@ -226,43 +198,37 @@ def tile_shifted_power_steps_t2_kernel(tc, x, a_words, a_scales, g, out_0, out_1
         copy_out(1, 0)
         copy_out(1, 1)
         for c in range(G):
-            for k in range(1, G):
-                mx_pass(0, c, k)
+            mx_pass(0, c, 1)
+        for c in range(G):
+            mx_pass(0, c, 2)
         quantize(1, 0)
         quantize(1, 1)
         sort_x(2)
         evac(0, 0)
         round_bf16(0, 0)
         evac(0, 1)
-        for n in range(1, slots):
-            more = n + 1 < slots
-            late = more and ORDER[n + 1][0] == ORDER[n - 1][0]
-            prev_late = n >= 2 and ORDER[n][0] == ORDER[n - 2][0]
-            if more and not late:
+        for n in range(1, slots - 1):
+            late = ORDER[n + 1][0] == ORDER[n - 1][0]
+            if not late:
                 transposes(n + 1)
                 copy_out(n + 1, 0)
                 copy_out(n + 1, 1)
             evac(n - 1, 2)
+            store_y(n - 1, 1)
             round_bf16(n - 1, 1)
             round_bf16(n - 1, 2)
-            sum_y(n - 1, 1)
-            if FORM[ORDER[n - 1][0]][1] != "T":
-                store_y(n - 1, 1)
             mm(n, 0)
-            if more and not late:
+            if not late:
                 quantize(n + 1, 0)
                 quantize(n + 1, 1)
-            for c in range(G):
-                scale_x2(n - 1, c)
-            feed(n - 1, 2)
-            sum_y(n - 1, 2)
-            store_y(n - 1, 2)
+            add_x3(n - 1, 2)
+            scale_y(nc.gpsimd, n - 1, 2)
             if n == 1:
                 sort_x(3)
-            feed(n, 0)
+            add_x3(n, 0)
+            scale_y(nc.gpsimd, n, 0)
             evac(n, 0)
-            if FORM[ORDER[n][0]][0] == "T":
-                store_y(n, 0)
+            store_y(n - 1, 2)
             round_bf16(n, 0)
             mm(n, 1)
             if late:
@@ -273,21 +239,31 @@ def tile_shifted_power_steps_t2_kernel(tc, x, a_words, a_scales, g, out_0, out_1
                 mm(n, 2)
                 quantize(n + 1, 0)
                 quantize(n + 1, 1)
-                feed(n, 1)
+                add_x3(n, 1)
+                scale_y(nc.gpsimd, n, 1)
             else:
-                feed(n, 1)
+                add_x3(n, 1)
+                scale_y(nc.gpsimd, n, 1)
                 evac(n, 1)
                 mm(n, 2)
-            if FORM[ORDER[n][0]][1] == "T":
-                store_y(n, 1)
-            sum_y(n, 0)
-            if FORM[ORDER[n][0]][0] != "T":
-                store_y(n, 0)
-        n = slots
-        feed(n - 1, 2)
+            store_y(n, 0)
+        n = slots - 1
+        add_x3(n - 1, 2)
+        scale_y(nc.gpsimd, n - 1, 2)
         evac(n - 1, 2)
-        sum_y(n - 1, 1)
-        if FORM[ORDER[n - 1][0]][1] != "T":
-            store_y(n - 1, 1)
-        sum_y(n - 1, 2)
+        store_y(n - 1, 1)
+        for c in range(G):
+            mm(n, c)
+        add_x3(n, 0)
+        scale_y(nc.gpsimd, n, 0)
+        evac(n, 0)
+        evac(n, 1)
         store_y(n - 1, 2)
+        add_x3(n, 1)
+        evac(n, 2)
+        add_x3(n, 2)
+        scale_y(nc.vector, n, 1)
+        store_y(n, 0)
+        store_y(n, 1)
+        scale_y(nc.vector, n, 2)
+        store_y(n, 2)

@@ -29,8 +29,8 @@ def tile_shifted_power_steps_t2_kernel(tc, x, a_words, a_scales, g, out_0, out_1
     with ExitStack() as ctx:
         keep = ctx.enter_context(tc.tile_pool(name="keep", bufs=1))
         work = ctx.enter_context(tc.tile_pool(name="work", bufs=1))
-        acc_pool = ctx.enter_context(tc.psum_pool(name="acc", bufs=6))
-        turn_pool = ctx.enter_context(tc.psum_pool(name="turn", bufs=2))
+        acc_pool = ctx.enter_context(tc.psum_pool(name="acc", bufs=5))
+        turn_pool = ctx.enter_context(tc.psum_pool(name="turn", bufs=3))
         ctx.enter_context(tc.manual_schedule())
 
         ident = keep.tile([P, P], F32, name="ident")
@@ -94,32 +94,48 @@ def tile_shifted_power_steps_t2_kernel(tc, x, a_words, a_scales, g, out_0, out_1
                 rounded[(i, 1, c)] = t
                 resid[(i, 1, c)] = t
 
-        def transposes(n):
-            i, s = ORDER[n]
-            banks = [turn_pool.tile([P, 4, P], F32, name="turn") for h in range(2)]
-            turned[n] = banks
-            for k in range(G):
-                words = rounded[(i, s, k)][:].bitcast(F32)
-                for u in range(2):
-                    nc.tensor.transpose(banks[min(k, 1)][:, 2 * (k // 2) + u, :], words[:, u * P : (u + 1) * P], ident[:])
+        def banks_of(run):
+            groups = [(n, k) for n in run for k in range(G)]
+            if len(run) == 1:
+                return [groups[:1], groups[1:]]
+            return [groups[j : j + 2] for j in range(0, len(groups), 2)]
 
-        def copy_out(n, h):
-            groups = 1 + h
-            t = work.tile([P, groups * W], BF16, name="grouped%d" % h, bufs=2, align_bytes=64)
-            grouped[(n, h)] = t
+        def transposes(run):
+            for groups in banks_of(run):
+                bank = turn_pool.tile([P, 4, P], F32, name="turn")
+                turned[groups[0]] = bank
+                for j, (n, k) in enumerate(groups):
+                    i, s = ORDER[n]
+                    words = rounded[(i, s, k)][:].bitcast(F32)
+                    for u in range(2):
+                        nc.tensor.transpose(bank[:, 2 * j + u, :], words[:, u * P : (u + 1) * P], ident[:])
+
+        def copy_out(groups):
+            t = work.tile([P, len(groups) * W], BF16, name="grouped", bufs=4, align_bytes=64)
+            grouped[groups[0]] = t
             nc.scalar.copy(
-                out=t[:].bitcast(F32).rearrange("p (k r u) -> p k r u", k=groups, u=2),
-                in_=turned[n][h][:, 0 : 2 * groups, :].rearrange("p (k u) r -> p k r u", u=2),
+                out=t[:].bitcast(F32).rearrange("p (k r u) -> p k r u", k=len(groups), u=2),
+                in_=turned[groups[0]][:, 0 : 2 * len(groups), :].rearrange("p (k u) r -> p k r u", u=2),
             )
 
-        def quantize(n, h):
-            groups = 1 + h
-            cd = work.tile([P, groups * P], U32, name="codes%d" % h, bufs=3, align_bytes=64)
-            sc = work.tile([P, groups * P], U8, name="scales%d" % h, bufs=3, align_bytes=64)
-            nc.vector.quantize_mx(out=cd[:].bitcast(FP8X4), scales=sc[:], in_=grouped[(n, h)][:])
-            for j in range(groups):
-                codes[(n, h + j)] = cd[:, j * P : (j + 1) * P]
-                scales[(n, h + j)] = sc[:, j * P : (j + 1) * P]
+        def quantize(groups):
+            cd = work.tile([P, len(groups) * P], U32, name="codes", bufs=6, align_bytes=64)
+            sc = work.tile([P, len(groups) * P], U8, name="scales", bufs=6, align_bytes=64)
+            nc.vector.quantize_mx(out=cd[:].bitcast(FP8X4), scales=sc[:], in_=grouped[groups[0]][:])
+            for j, group in enumerate(groups):
+                codes[group] = cd[:, j * P : (j + 1) * P]
+                scales[group] = sc[:, j * P : (j + 1) * P]
+
+        def turn(run):
+            transposes(run)
+            for groups in banks_of(run):
+                copy_out(groups)
+
+        def quantize_run(run):
+            for groups in banks_of(run):
+                quantize(groups)
+
+        RUNS = {2: [2], 3: [3], 4: [4, 5], 6: [6, 7], 8: [8], 9: [9], 10: [10], 11: [11]}
 
         def mx_pass(n, c, k):
             if k == 0:
@@ -186,59 +202,52 @@ def tile_shifted_power_steps_t2_kernel(tc, x, a_words, a_scales, g, out_0, out_1
 
         slots = len(ORDER)
         sort_x(0)
-        transposes(0)
-        copy_out(0, 0)
-        copy_out(0, 1)
-        quantize(0, 0)
-        quantize(0, 1)
+        turn([0])
+        quantize_run([0])
         sort_x(1)
         for c in range(G):
             mx_pass(0, c, 0)
-        transposes(1)
-        copy_out(1, 0)
-        copy_out(1, 1)
+        turn([1])
         for c in range(G):
             mx_pass(0, c, 1)
         for c in range(G):
             mx_pass(0, c, 2)
-        quantize(1, 0)
-        quantize(1, 1)
-        sort_x(2)
+        quantize_run([1])
         evac(0, 0)
         round_bf16(0, 0)
+        sort_x(2)
         evac(0, 1)
         for n in range(1, slots - 1):
             late = ORDER[n + 1][0] == ORDER[n - 1][0]
-            if not late:
-                transposes(n + 1)
-                copy_out(n + 1, 0)
-                copy_out(n + 1, 1)
+            if not late and n > 1:
+                turn(RUNS.get(n + 1, []))
             evac(n - 1, 2)
             store_y(n - 1, 1)
             round_bf16(n - 1, 1)
             round_bf16(n - 1, 2)
             mm(n, 0)
+            if n == 1:
+                turn([2])
+            if ORDER[n][1] < 3:
+                evac(n, 0)
+                round_bf16(n, 0)
             if not late:
-                quantize(n + 1, 0)
-                quantize(n + 1, 1)
+                quantize_run(RUNS.get(n + 1, []))
             add_x3(n - 1, 2)
             scale_y(nc.gpsimd, n - 1, 2)
-            if n == 1:
+            if n == 2:
                 sort_x(3)
             add_x3(n, 0)
             scale_y(nc.gpsimd, n, 0)
-            evac(n, 0)
+            if ORDER[n][1] == 3:
+                evac(n, 0)
             store_y(n - 1, 2)
-            round_bf16(n, 0)
             mm(n, 1)
             if late:
-                transposes(n + 1)
-                copy_out(n + 1, 0)
-                copy_out(n + 1, 1)
+                turn(RUNS.get(n + 1, []))
                 evac(n, 1)
                 mm(n, 2)
-                quantize(n + 1, 0)
-                quantize(n + 1, 1)
+                quantize_run(RUNS.get(n + 1, []))
                 add_x3(n, 1)
                 scale_y(nc.gpsimd, n, 1)
             else:

@@ -20,6 +20,7 @@ P = 128
 W = 512
 G = N // W
 TILES = M // P
+EARLY = 2
 
 ORDER = [(0, 1), (1, 1), (2, 1), (0, 2), (1, 2), (3, 1), (0, 3), (2, 2), (1, 3), (3, 2), (2, 3), (3, 3)]
 
@@ -56,11 +57,11 @@ def tile_shifted_power_steps_t2_kernel(tc, x, a_words, a_scales, g, out_0, out_1
             nc.sync.dma_start(out=a_codes[k][:].bitcast(I32), in_=a_words[k].bitcast(I32))
 
         load_x(0)
+        load_x(1)
         scale_rows = a_scales.bitcast(I32).rearrange("k (q r) n -> r q k n", r=4)
         for r in range(4):
             nc.sync.dma_start(out=a_plane0[r:P:32, :].bitcast(I32), in_=scale_rows[r][:, 0, :])
         load_a(0)
-        load_x(1)
         for r in range(4):
             nc.sync.dma_start(
                 out=a_plane12[r:P:32, :].bitcast(I32).rearrange("q (k n) -> q k n", k=2), in_=scale_rows[r][:, 1:G, :]
@@ -135,7 +136,7 @@ def tile_shifted_power_steps_t2_kernel(tc, x, a_words, a_scales, g, out_0, out_1
             for groups in banks_of(run):
                 quantize(groups)
 
-        RUNS = {2: [2], 3: [3], 4: [4, 5], 6: [6, 7], 8: [8], 9: [9], 10: [10], 11: [11]}
+        RUNS = {2: [2], 3: [3], 4: [4, 5], 6: [6, 7], 8: [8, 9], 10: [10], 11: [11]}
 
         def mx_pass(n, c, k):
             if k == 0:
@@ -151,7 +152,7 @@ def tile_shifted_power_steps_t2_kernel(tc, x, a_words, a_scales, g, out_0, out_1
             )
 
         def mm(n, c):
-            for k in range(G):
+            for k in range(1 if n == 1 and c < EARLY else 0, G):
                 mx_pass(n, c, k)
 
         def evac(n, c):
@@ -203,16 +204,17 @@ def tile_shifted_power_steps_t2_kernel(tc, x, a_words, a_scales, g, out_0, out_1
         slots = len(ORDER)
         sort_x(0)
         turn([0])
-        quantize_run([0])
         sort_x(1)
+        quantize_run([0])
+        turn([1])
+        quantize_run([1])
         for c in range(G):
             mx_pass(0, c, 0)
-        turn([1])
-        for c in range(G):
-            mx_pass(0, c, 1)
-        for c in range(G):
-            mx_pass(0, c, 2)
-        quantize_run([1])
+        for c in range(EARLY):
+            mx_pass(1, c, 0)
+        for k in range(1, G):
+            for c in range(G):
+                mx_pass(0, c, k)
         evac(0, 0)
         round_bf16(0, 0)
         sort_x(2)
@@ -228,11 +230,14 @@ def tile_shifted_power_steps_t2_kernel(tc, x, a_words, a_scales, g, out_0, out_1
             mm(n, 0)
             if n == 1:
                 turn([2])
+            banks = [] if late else banks_of(RUNS.get(n + 1, []))
+            for groups in banks[:-2]:
+                quantize(groups)
             if ORDER[n][1] < 3:
                 evac(n, 0)
                 round_bf16(n, 0)
-            if not late:
-                quantize_run(RUNS.get(n + 1, []))
+            for groups in banks[-2:]:
+                quantize(groups)
             add_x3(n - 1, 2)
             scale_y(nc.gpsimd, n - 1, 2)
             if n == 2:

@@ -18,266 +18,269 @@ MULT = mybir.AluOpType.mult
 
 P = 128
 W = 512
-G = N // W
+GROUPS = N // W
 TILES = M // P
-EARLY = 2
 
-ORDER = [(0, 1), (1, 1), (2, 1), (0, 2), (1, 2), (3, 1), (0, 3), (2, 2), (1, 3), (3, 2), (2, 3), (3, 3)]
+TURN_BANKS = 3
+SUM_BANKS = 5
+EARLY_BANKS = SUM_BANKS - GROUPS
+
+STEPS = [(0, 1), (1, 1), (2, 1), (0, 2), (1, 2), (3, 1), (0, 3), (2, 2), (1, 3), (3, 2), (2, 3), (3, 3)]
+LAST = len(STEPS) - 1
+
+
+def transpose_runs():
+    runs = {}
+    joined = set()
+    for n in range(2, len(STEPS)):
+        if n not in joined:
+            runs[n] = [n]
+            if n < LAST:
+                i, number = STEPS[n + 1]
+                if number == 1 or STEPS.index((i, number - 1)) <= n - 3:
+                    runs[n].append(n + 1)
+                    joined.add(n + 1)
+    return runs
+
+
+def banks_of(run):
+    operands = [(n, j) for n in run for j in range(GROUPS)]
+    if len(run) == 1:
+        return [operands[:1], operands[1:]]
+    return [operands[first : first + 2] for first in range(0, len(operands), 2)]
 
 
 def tile_shifted_power_steps_t2_kernel(tc, x, a_words, a_scales, g, out_0, out_1):
     nc = tc.nc
+    runs = transpose_runs()
     with ExitStack() as ctx:
         keep = ctx.enter_context(tc.tile_pool(name="keep", bufs=1))
         work = ctx.enter_context(tc.tile_pool(name="work", bufs=1))
-        acc_pool = ctx.enter_context(tc.psum_pool(name="acc", bufs=5))
-        turn_pool = ctx.enter_context(tc.psum_pool(name="turn", bufs=3))
+        sum_pool = ctx.enter_context(tc.psum_pool(name="sums", bufs=SUM_BANKS))
+        turn_pool = ctx.enter_context(tc.psum_pool(name="turn", bufs=TURN_BANKS))
         ctx.enter_context(tc.manual_schedule())
 
         ident = keep.tile([P, P], F32, name="ident")
-        a_plane0 = keep.tile([P, N], U8, name="a_plane0", align_bytes=64)
-        a_plane12 = keep.tile([P, 2 * N], U8, name="a_plane12", align_bytes=64)
-        a_plane = [a_plane0[:], a_plane12[:, 0:N], a_plane12[:, N : 2 * N]]
-        a_codes = [keep.tile([P, 2 * N], U8, name="a_codes%d" % k, align_bytes=64) for k in range(G)]
+        a_scale_first = keep.tile([P, N], U8, name="a_scale_first", align_bytes=64)
+        a_scale_rest = keep.tile([P, (GROUPS - 1) * N], U8, name="a_scale_rest", align_bytes=64)
+        a_scale = [a_scale_first[:]] + [a_scale_rest[:, j * N : (j + 1) * N] for j in range(GROUPS - 1)]
+        a_codes = [keep.tile([P, 2 * N], U8, name="a_codes%d" % j, align_bytes=64) for j in range(GROUPS)]
         x_raw = [keep.tile([P, N], BF16, name="x_raw%d" % i) for i in range(TILES)]
-        g_nat = keep.tile([P, N], BF16, name="g_nat")
-        warm = keep.tile([P, 8], F32, name="warm")
-        warm2 = keep.tile([P, 8], F32, name="warm2")
+        gain = keep.tile([P, N], BF16, name="gain")
 
-        nc.gpsimd.memset(warm[:], 0.0)
         make_identity(nc, ident[:])
-        nc.scalar.copy(out=warm2[:], in_=warm[:])
-        nc.vector.memset(a_plane0[:].bitcast(I32), 0)
-        nc.vector.memset(a_plane12[:].bitcast(I32), 0)
+        nc.vector.memset(a_scale_first[:].bitcast(I32), 0)
+        nc.vector.memset(a_scale_rest[:].bitcast(I32), 0)
 
         def load_x(i):
             nc.sync.dma_start(out=x_raw[i][:], in_=x[i * P : (i + 1) * P, :])
 
-        def load_a(k):
-            nc.sync.dma_start(out=a_codes[k][:].bitcast(I32), in_=a_words[k].bitcast(I32))
+        def load_a(j):
+            nc.sync.dma_start(out=a_codes[j][:].bitcast(I32), in_=a_words[j].bitcast(I32))
 
         load_x(0)
         load_x(1)
-        scale_rows = a_scales.bitcast(I32).rearrange("k (q r) n -> r q k n", r=4)
+        scale_rows = a_scales.bitcast(I32).rearrange("j (q r) n -> r q j n", r=4)
         for r in range(4):
-            nc.sync.dma_start(out=a_plane0[r:P:32, :].bitcast(I32), in_=scale_rows[r][:, 0, :])
+            nc.sync.dma_start(out=a_scale_first[r:P:32, :].bitcast(I32), in_=scale_rows[r][:, 0, :])
         load_a(0)
         for r in range(4):
             nc.sync.dma_start(
-                out=a_plane12[r:P:32, :].bitcast(I32).rearrange("q (k n) -> q k n", k=2), in_=scale_rows[r][:, 1:G, :]
+                out=a_scale_rest[r:P:32, :].bitcast(I32).rearrange("q (j n) -> q j n", j=GROUPS - 1),
+                in_=scale_rows[r][:, 1:GROUPS, :],
             )
         load_a(1)
         load_a(2)
         load_x(2)
         load_x(3)
-        nc.sync.dma_start(out=g_nat[:], in_=g.partition_broadcast(P))
-
-        def sort_words(dst, src):
-            nc.vector.tensor_copy(
-                out=dst.bitcast(F32).rearrange("t (u p) -> t u p", u=2),
-                in_=src.bitcast(F32).rearrange("t (p u) -> t u p", u=2),
-            )
+        nc.sync.dma_start(out=gain[:], in_=g.partition_broadcast(P))
 
         rounded = {}
-        resid = {}
+        exact = {}
         turned = {}
-        grouped = {}
+        packed = {}
         codes = {}
         scales = {}
-        acc = {}
+        sums = {}
         x3 = {}
         y = {}
 
         def sort_x(i):
-            for c in range(G):
-                t = work.tile([P, W], BF16, name="x_sorted", bufs=TILES * G)
-                sort_words(t[:], x_raw[i][:, c * W : (c + 1) * W])
-                rounded[(i, 1, c)] = t
-                resid[(i, 1, c)] = t
-
-        def banks_of(run):
-            groups = [(n, k) for n in run for k in range(G)]
-            if len(run) == 1:
-                return [groups[:1], groups[1:]]
-            return [groups[j : j + 2] for j in range(0, len(groups), 2)]
-
-        def transposes(run):
-            for groups in banks_of(run):
-                bank = turn_pool.tile([P, 4, P], F32, name="turn")
-                turned[groups[0]] = bank
-                for j, (n, k) in enumerate(groups):
-                    i, s = ORDER[n]
-                    words = rounded[(i, s, k)][:].bitcast(F32)
-                    for u in range(2):
-                        nc.tensor.transpose(bank[:, 2 * j + u, :], words[:, u * P : (u + 1) * P], ident[:])
-
-        def copy_out(groups):
-            t = work.tile([P, len(groups) * W], BF16, name="grouped", bufs=4, align_bytes=64)
-            grouped[groups[0]] = t
-            nc.scalar.copy(
-                out=t[:].bitcast(F32).rearrange("p (k r u) -> p k r u", k=len(groups), u=2),
-                in_=turned[groups[0]][:, 0 : 2 * len(groups), :].rearrange("p (k u) r -> p k r u", u=2),
-            )
-
-        def quantize(groups):
-            cd = work.tile([P, len(groups) * P], U32, name="codes", bufs=6, align_bytes=64)
-            sc = work.tile([P, len(groups) * P], U8, name="scales", bufs=6, align_bytes=64)
-            nc.vector.quantize_mx(out=cd[:].bitcast(FP8X4), scales=sc[:], in_=grouped[groups[0]][:])
-            for j, group in enumerate(groups):
-                codes[group] = cd[:, j * P : (j + 1) * P]
-                scales[group] = sc[:, j * P : (j + 1) * P]
+            for j in range(GROUPS):
+                x_sorted = work.tile([P, W], BF16, name="x_sorted", bufs=TILES * GROUPS)
+                nc.vector.tensor_copy(
+                    out=x_sorted[:].bitcast(F32).rearrange("r (u p) -> r u p", u=2),
+                    in_=x_raw[i][:, j * W : (j + 1) * W].bitcast(F32).rearrange("r (p u) -> r u p", u=2),
+                )
+                rounded[(i, 1, j)] = x_sorted
+                exact[(i, 1, j)] = x_sorted
 
         def turn(run):
-            transposes(run)
-            for groups in banks_of(run):
-                copy_out(groups)
+            for operands in banks_of(run):
+                bank = turn_pool.tile([P, 4, P], F32, name="turn")
+                turned[operands[0]] = bank
+                for place, (n, j) in enumerate(operands):
+                    pairs = rounded[STEPS[n] + (j,)][:].bitcast(F32)
+                    for u in range(2):
+                        nc.tensor.transpose(bank[:, 2 * place + u, :], pairs[:, u * P : (u + 1) * P], ident[:])
+            for operands in banks_of(run):
+                count = len(operands)
+                quads = work.tile([P, count * W], BF16, name="quads", bufs=4, align_bytes=64)
+                packed[operands[0]] = quads
+                nc.scalar.copy(
+                    out=quads[:].bitcast(F32).rearrange("p (j r u) -> p j r u", j=count, u=2),
+                    in_=turned[operands[0]][:, 0 : 2 * count, :].rearrange("p (j u) r -> p j r u", u=2),
+                )
 
-        def quantize_run(run):
-            for groups in banks_of(run):
-                quantize(groups)
+        def quantize(banks):
+            for operands in banks:
+                count = len(operands)
+                words = work.tile([P, count * P], U32, name="words", bufs=6, align_bytes=64)
+                exponents = work.tile([P, count * P], U8, name="exponents", bufs=6, align_bytes=64)
+                nc.vector.quantize_mx(out=words[:].bitcast(FP8X4), scales=exponents[:], in_=packed[operands[0]][:])
+                for place, operand in enumerate(operands):
+                    codes[operand] = words[:, place * P : (place + 1) * P]
+                    scales[operand] = exponents[:, place * P : (place + 1) * P]
 
-        RUNS = {2: [2], 3: [3], 4: [4, 5], 6: [6, 7], 8: [8, 9], 10: [10], 11: [11]}
-
-        def mx_pass(n, c, k):
-            if k == 0:
-                acc[(n, c)] = acc_pool.tile([P, W], F32, name="acc")
+        def mx_pass(n, c, j):
+            if j == 0:
+                sums[(n, c)] = sum_pool.tile([P, W], F32, name="sums")
             nc.tensor.matmul_mx(
-                out=acc[(n, c)][:],
-                lhsT=codes[(n, k)].bitcast(FP8X4),
-                lhsT_scale=scales[(n, k)],
-                rhs=a_codes[k][:, 2 * W * c : 2 * W * (c + 1)].bitcast(FP4X4),
-                rhs_scale=a_plane[k][:, c * W : (c + 1) * W],
-                start=(k == 0),
-                stop=(k == G - 1),
+                out=sums[(n, c)][:],
+                lhsT=codes[(n, j)].bitcast(FP8X4),
+                lhsT_scale=scales[(n, j)],
+                rhs=a_codes[j][:, 2 * W * c : 2 * W * (c + 1)].bitcast(FP4X4),
+                rhs_scale=a_scale[j][:, c * W : (c + 1) * W],
+                start=(j == 0),
+                stop=(j == GROUPS - 1),
             )
 
-        def mm(n, c):
-            for k in range(1 if n == 1 and c < EARLY else 0, G):
-                mx_pass(n, c, k)
+        def multiply(n, c):
+            for j in range(1 if (n, c) in sums else 0, GROUPS):
+                mx_pass(n, c, j)
 
-        def evac(n, c):
-            i, s = ORDER[n]
-            if s < 3:
-                t = work.tile([P, W], F32, name="iterate", bufs=15)
+        def read_sum(n, c):
+            i, number = STEPS[n]
+            if number < 3:
+                iterate = work.tile([P, W], F32, name="iterate", bufs=5 * GROUPS)
                 nc.vector.tensor_tensor(
-                    out=t[:].rearrange("t (u p e) -> t u p e", u=2, e=2),
-                    in0=acc[(n, c)][:].rearrange("t (p u e) -> t u p e", u=2, e=2),
-                    in1=resid[(i, s, c)][:].rearrange("t (u p e) -> t u p e", u=2, e=2),
+                    out=iterate[:].rearrange("r (u p e) -> r u p e", u=2, e=2),
+                    in0=sums[(n, c)][:].rearrange("r (p u e) -> r u p e", u=2, e=2),
+                    in1=exact[(i, number, c)][:].rearrange("r (u p e) -> r u p e", u=2, e=2),
                     op=ADD,
                 )
-                resid[(i, s + 1, c)] = t
+                exact[(i, number + 1, c)] = iterate
             else:
-                t = work.tile([P, W], F32, name="move", bufs=6)
-                nc.vector.tensor_tensor(out=t[:], in0=acc[(n, c)][:], in1=g_nat[:, c * W : (c + 1) * W], op=MULT)
-                nc.sync.dma_start(out=out_1[i * P : (i + 1) * P, c * W : (c + 1) * W], in_=t[:])
+                move = work.tile([P, W], F32, name="move", bufs=2 * GROUPS)
+                nc.vector.tensor_tensor(out=move[:], in0=sums[(n, c)][:], in1=gain[:, c * W : (c + 1) * W], op=MULT)
+                nc.sync.dma_start(out=out_1[i * P : (i + 1) * P, c * W : (c + 1) * W], in_=move[:])
 
         def round_bf16(n, c):
-            i, s = ORDER[n]
-            if s < 3:
-                t = work.tile([P, W], BF16, name="rounded", bufs=9)
-                nc.scalar.copy(out=t[:], in_=resid[(i, s + 1, c)][:])
-                rounded[(i, s + 1, c)] = t
+            i, number = STEPS[n]
+            if number < 3:
+                narrow = work.tile([P, W], BF16, name="narrow", bufs=3 * GROUPS)
+                nc.scalar.copy(out=narrow[:], in_=exact[(i, number + 1, c)][:])
+                rounded[(i, number + 1, c)] = narrow
 
         def add_x3(n, c):
-            i, s = ORDER[n]
-            if s == 3:
-                t = work.tile([P, W], F32, name="x3", bufs=6)
+            i, number = STEPS[n]
+            if number == 3:
+                total = work.tile([P, W], F32, name="total", bufs=2 * GROUPS)
                 nc.vector.tensor_tensor(
-                    out=t[:].rearrange("t (p u e) -> t p u e", u=2, e=2),
-                    in0=acc[(n, c)][:].rearrange("t (p u e) -> t p u e", u=2, e=2),
-                    in1=resid[(i, 3, c)][:].rearrange("t (u p e) -> t p u e", u=2, e=2),
+                    out=total[:].rearrange("r (p u e) -> r p u e", u=2, e=2),
+                    in0=sums[(n, c)][:].rearrange("r (p u e) -> r p u e", u=2, e=2),
+                    in1=exact[(i, 3, c)][:].rearrange("r (u p e) -> r p u e", u=2, e=2),
                     op=ADD,
                 )
-                x3[(n, c)] = t
+                x3[(n, c)] = total
 
         def scale_y(engine, n, c):
-            if ORDER[n][1] == 3:
-                t = work.tile([P, W], F32, name="y", bufs=6)
-                engine.tensor_tensor(out=t[:], in0=x3[(n, c)][:], in1=g_nat[:, c * W : (c + 1) * W], op=MULT)
-                y[(n, c)] = t
+            if STEPS[n][1] == 3:
+                scaled = work.tile([P, W], F32, name="scaled", bufs=2 * GROUPS)
+                engine.tensor_tensor(out=scaled[:], in0=x3[(n, c)][:], in1=gain[:, c * W : (c + 1) * W], op=MULT)
+                y[(n, c)] = scaled
 
         def store_y(n, c):
-            i, s = ORDER[n]
-            if s == 3:
+            i, number = STEPS[n]
+            if number == 3:
                 nc.sync.dma_start(out=out_0[i * P : (i + 1) * P, c * W : (c + 1) * W], in_=y[(n, c)][:])
 
-        slots = len(ORDER)
         sort_x(0)
         turn([0])
         sort_x(1)
-        quantize_run([0])
+        quantize(banks_of([0]))
         turn([1])
-        quantize_run([1])
-        for c in range(G):
+        quantize(banks_of([1]))
+        for c in range(GROUPS):
             mx_pass(0, c, 0)
-        for c in range(EARLY):
+        for c in range(EARLY_BANKS):
             mx_pass(1, c, 0)
-        for k in range(1, G):
-            for c in range(G):
-                mx_pass(0, c, k)
-        evac(0, 0)
+        for j in range(1, GROUPS):
+            for c in range(GROUPS):
+                mx_pass(0, c, j)
+        read_sum(0, 0)
         round_bf16(0, 0)
         sort_x(2)
-        evac(0, 1)
-        for n in range(1, slots - 1):
-            late = ORDER[n + 1][0] == ORDER[n - 1][0]
-            if not late and n > 1:
-                turn(RUNS.get(n + 1, []))
-            evac(n - 1, 2)
+        read_sum(0, 1)
+
+        for n in range(1, LAST):
+            run = runs.get(n + 1, [])
+            late = STEPS[n + 1][0] == STEPS[n - 1][0]
+            behind_a = n == 1
+            if not late and not behind_a:
+                turn(run)
+            read_sum(n - 1, 2)
             store_y(n - 1, 1)
+            multiply(n, 0)
+            if behind_a:
+                turn(run)
             round_bf16(n - 1, 1)
             round_bf16(n - 1, 2)
-            mm(n, 0)
-            if n == 1:
-                turn([2])
-            banks = [] if late else banks_of(RUNS.get(n + 1, []))
-            for groups in banks[:-2]:
-                quantize(groups)
-            if ORDER[n][1] < 3:
-                evac(n, 0)
+            banks = [] if late else banks_of(run)
+            quantize(banks[:-2])
+            if STEPS[n][1] < 3:
+                read_sum(n, 0)
                 round_bf16(n, 0)
-            for groups in banks[-2:]:
-                quantize(groups)
+            quantize(banks[-2:])
             add_x3(n - 1, 2)
             scale_y(nc.gpsimd, n - 1, 2)
-            if n == 2:
-                sort_x(3)
+            if STEPS.index((TILES - 1, 1)) in runs.get(n + 2, []):
+                sort_x(TILES - 1)
             add_x3(n, 0)
             scale_y(nc.gpsimd, n, 0)
-            if ORDER[n][1] == 3:
-                evac(n, 0)
+            if STEPS[n][1] == 3:
+                read_sum(n, 0)
             store_y(n - 1, 2)
-            mm(n, 1)
+            multiply(n, 1)
             if late:
-                turn(RUNS.get(n + 1, []))
-                evac(n, 1)
-                mm(n, 2)
-                quantize_run(RUNS.get(n + 1, []))
+                turn(run)
+                read_sum(n, 1)
+                multiply(n, 2)
+                quantize(banks_of(run))
                 add_x3(n, 1)
                 scale_y(nc.gpsimd, n, 1)
             else:
                 add_x3(n, 1)
                 scale_y(nc.gpsimd, n, 1)
-                evac(n, 1)
-                mm(n, 2)
+                read_sum(n, 1)
+                multiply(n, 2)
             store_y(n, 0)
-        n = slots - 1
-        add_x3(n - 1, 2)
-        scale_y(nc.gpsimd, n - 1, 2)
-        evac(n - 1, 2)
-        store_y(n - 1, 1)
-        for c in range(G):
-            mm(n, c)
-        add_x3(n, 0)
-        scale_y(nc.gpsimd, n, 0)
-        evac(n, 0)
-        evac(n, 1)
-        store_y(n - 1, 2)
-        add_x3(n, 1)
-        evac(n, 2)
-        add_x3(n, 2)
-        scale_y(nc.vector, n, 1)
-        store_y(n, 0)
-        store_y(n, 1)
-        scale_y(nc.vector, n, 2)
-        store_y(n, 2)
+
+        read_sum(LAST - 1, 2)
+        add_x3(LAST - 1, 2)
+        scale_y(nc.gpsimd, LAST - 1, 2)
+        store_y(LAST - 1, 1)
+        for c in range(GROUPS):
+            multiply(LAST, c)
+        read_sum(LAST, 0)
+        add_x3(LAST, 0)
+        scale_y(nc.gpsimd, LAST, 0)
+        read_sum(LAST, 1)
+        store_y(LAST - 1, 2)
+        add_x3(LAST, 1)
+        read_sum(LAST, 2)
+        add_x3(LAST, 2)
+        store_y(LAST, 0)
+        for c in range(1, GROUPS):
+            scale_y(nc.vector, LAST, c)
+            store_y(LAST, c)

from contextlib import ExitStack

import concourse.mybir as mybir
from concourse.masks import make_identity

M, N = 512, 1536
FLOPS = 3 * 2 * M * N * N

F32 = mybir.dt.float32
BF16 = mybir.dt.bfloat16
I32 = mybir.dt.int32
U32 = mybir.dt.uint32
U8 = mybir.dt.uint8
FP8X4 = mybir.dt.float8_e4m3fn_x4
FP4X4 = mybir.dt.float4_e2m1fn_x4
ADD = mybir.AluOpType.add
MULT = mybir.AluOpType.mult

P = 128
W = 512
GROUPS = N // W
TILES = M // P

TURN_BANKS = 3
SUM_BANKS = 5
EARLY_BANKS = SUM_BANKS - GROUPS

STEPS = [(0, 1), (1, 1), (2, 1), (0, 2), (1, 2), (3, 1), (0, 3), (2, 2), (1, 3), (3, 2), (2, 3), (3, 3)]
LAST = len(STEPS) - 1


def transpose_runs():
    runs = {}
    joined = set()
    for n in range(2, len(STEPS)):
        if n not in joined:
            runs[n] = [n]
            if n < LAST:
                i, number = STEPS[n + 1]
                if number == 1 or STEPS.index((i, number - 1)) <= n - 3:
                    runs[n].append(n + 1)
                    joined.add(n + 1)
    return runs


def banks_of(run):
    operands = [(n, j) for n in run for j in range(GROUPS)]
    if len(run) == 1:
        return [operands[:1], operands[1:]]
    return [operands[first : first + 2] for first in range(0, len(operands), 2)]


def tile_shifted_power_steps_t2_kernel(tc, x, a_words, a_scales, g, out_0, out_1):
    nc = tc.nc
    runs = transpose_runs()
    with ExitStack() as ctx:
        keep = ctx.enter_context(tc.tile_pool(name="keep", bufs=1))
        work = ctx.enter_context(tc.tile_pool(name="work", bufs=1))
        sum_pool = ctx.enter_context(tc.psum_pool(name="sums", bufs=SUM_BANKS))
        turn_pool = ctx.enter_context(tc.psum_pool(name="turn", bufs=TURN_BANKS))
        ctx.enter_context(tc.manual_schedule())

        ident = keep.tile([P, P], F32, name="ident")
        a_scale_first = keep.tile([P, N], U8, name="a_scale_first", align_bytes=64)
        a_scale_rest = keep.tile([P, (GROUPS - 1) * N], U8, name="a_scale_rest", align_bytes=64)
        a_scale = [a_scale_first[:]] + [a_scale_rest[:, j * N : (j + 1) * N] for j in range(GROUPS - 1)]
        a_codes = [keep.tile([P, 2 * N], U8, name="a_codes%d" % j, align_bytes=64) for j in range(GROUPS)]
        x_raw = [keep.tile([P, N], BF16, name="x_raw%d" % i) for i in range(TILES)]
        gain = keep.tile([P, N], BF16, name="gain")

        make_identity(nc, ident[:])
        nc.vector.memset(a_scale_first[:].bitcast(I32), 0)
        nc.vector.memset(a_scale_rest[:].bitcast(I32), 0)

        def load_x(i):
            nc.sync.dma_start(out=x_raw[i][:], in_=x[i * P : (i + 1) * P, :])

        def load_a(j):
            nc.sync.dma_start(out=a_codes[j][:].bitcast(I32), in_=a_words[j].bitcast(I32))

        load_x(0)
        load_x(1)
        scale_rows = a_scales.bitcast(I32).rearrange("j (q r) n -> r q j n", r=4)
        for r in range(4):
            nc.sync.dma_start(out=a_scale_first[r:P:32, :].bitcast(I32), in_=scale_rows[r][:, 0, :])
        load_a(0)
        for r in range(4):
            nc.sync.dma_start(
                out=a_scale_rest[r:P:32, :].bitcast(I32).rearrange("q (j n) -> q j n", j=GROUPS - 1),
                in_=scale_rows[r][:, 1:GROUPS, :],
            )
        load_a(1)
        load_a(2)
        load_x(2)
        load_x(3)
        nc.sync.dma_start(out=gain[:], in_=g.partition_broadcast(P))

        rounded = {}
        exact = {}
        turned = {}
        packed = {}
        codes = {}
        scales = {}
        sums = {}
        x3 = {}
        y = {}

        def sort_x(i):
            for j in range(GROUPS):
                x_sorted = work.tile([P, W], BF16, name="x_sorted", bufs=TILES * GROUPS)
                nc.vector.tensor_copy(
                    out=x_sorted[:].bitcast(F32).rearrange("r (u p) -> r u p", u=2),
                    in_=x_raw[i][:, j * W : (j + 1) * W].bitcast(F32).rearrange("r (p u) -> r u p", u=2),
                )
                rounded[(i, 1, j)] = x_sorted
                exact[(i, 1, j)] = x_sorted

        def turn(run):
            for operands in banks_of(run):
                bank = turn_pool.tile([P, 4, P], F32, name="turn")
                turned[operands[0]] = bank
                for place, (n, j) in enumerate(operands):
                    pairs = rounded[STEPS[n] + (j,)][:].bitcast(F32)
                    for u in range(2):
                        nc.tensor.transpose(bank[:, 2 * place + u, :], pairs[:, u * P : (u + 1) * P], ident[:])
            for operands in banks_of(run):
                count = len(operands)
                quads = work.tile([P, count * W], BF16, name="quads", bufs=4, align_bytes=64)
                packed[operands[0]] = quads
                nc.scalar.copy(
                    out=quads[:].bitcast(F32).rearrange("p (j r u) -> p j r u", j=count, u=2),
                    in_=turned[operands[0]][:, 0 : 2 * count, :].rearrange("p (j u) r -> p j r u", u=2),
                )

        def quantize(banks):
            for operands in banks:
                count = len(operands)
                words = work.tile([P, count * P], U32, name="words", bufs=6, align_bytes=64)
                exponents = work.tile([P, count * P], U8, name="exponents", bufs=6, align_bytes=64)
                nc.vector.quantize_mx(out=words[:].bitcast(FP8X4), scales=exponents[:], in_=packed[operands[0]][:])
                for place, operand in enumerate(operands):
                    codes[operand] = words[:, place * P : (place + 1) * P]
                    scales[operand] = exponents[:, place * P : (place + 1) * P]

        def mx_pass(n, c, j):
            if j == 0:
                sums[(n, c)] = sum_pool.tile([P, W], F32, name="sums")
            nc.tensor.matmul_mx(
                out=sums[(n, c)][:],
                lhsT=codes[(n, j)].bitcast(FP8X4),
                lhsT_scale=scales[(n, j)],
                rhs=a_codes[j][:, 2 * W * c : 2 * W * (c + 1)].bitcast(FP4X4),
                rhs_scale=a_scale[j][:, c * W : (c + 1) * W],
                start=(j == 0),
                stop=(j == GROUPS - 1),
            )

        def multiply(n, c):
            for j in range(1 if (n, c) in sums else 0, GROUPS):
                mx_pass(n, c, j)

        def read_sum(n, c):
            i, number = STEPS[n]
            if number < 3:
                iterate = work.tile([P, W], F32, name="iterate", bufs=5 * GROUPS)
                nc.vector.tensor_tensor(
                    out=iterate[:].rearrange("r (u p e) -> r u p e", u=2, e=2),
                    in0=sums[(n, c)][:].rearrange("r (p u e) -> r u p e", u=2, e=2),
                    in1=exact[(i, number, c)][:].rearrange("r (u p e) -> r u p e", u=2, e=2),
                    op=ADD,
                )
                exact[(i, number + 1, c)] = iterate
            else:
                move = work.tile([P, W], F32, name="move", bufs=2 * GROUPS)
                nc.vector.tensor_tensor(out=move[:], in0=sums[(n, c)][:], in1=gain[:, c * W : (c + 1) * W], op=MULT)
                nc.sync.dma_start(out=out_1[i * P : (i + 1) * P, c * W : (c + 1) * W], in_=move[:])

        def round_bf16(n, c):
            i, number = STEPS[n]
            if number < 3:
                narrow = work.tile([P, W], BF16, name="narrow", bufs=3 * GROUPS)
                nc.scalar.copy(out=narrow[:], in_=exact[(i, number + 1, c)][:])
                rounded[(i, number + 1, c)] = narrow

        def add_x3(n, c):
            i, number = STEPS[n]
            if number == 3:
                total = work.tile([P, W], F32, name="total", bufs=2 * GROUPS)
                nc.vector.tensor_tensor(
                    out=total[:].rearrange("r (p u e) -> r p u e", u=2, e=2),
                    in0=sums[(n, c)][:].rearrange("r (p u e) -> r p u e", u=2, e=2),
                    in1=exact[(i, 3, c)][:].rearrange("r (u p e) -> r p u e", u=2, e=2),
                    op=ADD,
                )
                x3[(n, c)] = total

        def scale_y(engine, n, c):
            if STEPS[n][1] == 3:
                scaled = work.tile([P, W], F32, name="scaled", bufs=2 * GROUPS)
                engine.tensor_tensor(out=scaled[:], in0=x3[(n, c)][:], in1=gain[:, c * W : (c + 1) * W], op=MULT)
                y[(n, c)] = scaled

        def store_y(n, c):
            i, number = STEPS[n]
            if number == 3:
                nc.sync.dma_start(out=out_0[i * P : (i + 1) * P, c * W : (c + 1) * W], in_=y[(n, c)][:])

        sort_x(0)
        turn([0])
        sort_x(1)
        quantize(banks_of([0]))
        turn([1])
        quantize(banks_of([1]))
        for c in range(GROUPS):
            mx_pass(0, c, 0)
        for c in range(EARLY_BANKS):
            mx_pass(1, c, 0)
        for j in range(1, GROUPS):
            for c in range(GROUPS):
                mx_pass(0, c, j)
        read_sum(0, 0)
        round_bf16(0, 0)
        sort_x(2)
        read_sum(0, 1)

        for n in range(1, LAST):
            run = runs.get(n + 1, [])
            late = STEPS[n + 1][0] == STEPS[n - 1][0]
            behind_a = n == 1
            if not late and not behind_a:
                turn(run)
            read_sum(n - 1, 2)
            store_y(n - 1, 1)
            multiply(n, 0)
            if behind_a:
                turn(run)
            round_bf16(n - 1, 1)
            round_bf16(n - 1, 2)
            banks = [] if late else banks_of(run)
            quantize(banks[:-2])
            if STEPS[n][1] < 3:
                read_sum(n, 0)
                round_bf16(n, 0)
            quantize(banks[-2:])
            add_x3(n - 1, 2)
            scale_y(nc.gpsimd, n - 1, 2)
            if STEPS.index((TILES - 1, 1)) in runs.get(n + 2, []):
                sort_x(TILES - 1)
            add_x3(n, 0)
            scale_y(nc.gpsimd, n, 0)
            if STEPS[n][1] == 3:
                read_sum(n, 0)
            store_y(n - 1, 2)
            multiply(n, 1)
            if late:
                turn(run)
                read_sum(n, 1)
                multiply(n, 2)
                quantize(banks_of(run))
                add_x3(n, 1)
                scale_y(nc.gpsimd, n, 1)
            else:
                add_x3(n, 1)
                scale_y(nc.gpsimd, n, 1)
                read_sum(n, 1)
                multiply(n, 2)
            store_y(n, 0)

        read_sum(LAST - 1, 2)
        add_x3(LAST - 1, 2)
        scale_y(nc.gpsimd, LAST - 1, 2)
        store_y(LAST - 1, 1)
        for c in range(GROUPS):
            multiply(LAST, c)
        read_sum(LAST, 0)
        add_x3(LAST, 0)
        scale_y(nc.gpsimd, LAST, 0)
        read_sum(LAST, 1)
        store_y(LAST - 1, 2)
        add_x3(LAST, 1)
        read_sum(LAST, 2)
        add_x3(LAST, 2)
        store_y(LAST, 0)
        for c in range(1, GROUPS):
            scale_y(nc.vector, LAST, c)
            store_y(LAST, c)
